import numpy as np
import ml_dtypes


def mxq(x, axis, fmt="e4m3"):
    dtype, down = {"e4m3": (ml_dtypes.float8_e4m3fn, 7), "e5m2": (ml_dtypes.float8_e5m2, 14)}[fmt]
    v = np.moveaxis(np.asarray(x, np.float32).astype(ml_dtypes.bfloat16).astype(np.float64), axis, -1)
    blocks = v.reshape(v.shape[:-1] + (-1, 32))
    amax = np.abs(blocks).max(-1, keepdims=True)
    byte = np.maximum(np.where(amax > 0, np.frexp(amax)[1] - 1 + 127, 0) - down, 1)
    scale = np.exp2(byte - 127.0)
    codes = (blocks / scale).astype(np.float32).astype(dtype).astype(np.float64)
    return np.moveaxis((codes * scale).reshape(v.shape), -1, axis)


WIDE = False


def mx_kscale(k):
    if not WIDE:
        return np.ones(k)
    levels = np.array([10, -10, 5, -5, 0])
    if k % 512:
        return np.exp2(np.random.permutation(np.resize(levels, k // 32))).repeat(32)
    a = np.empty((k // 512, 16))
    for p in range(k // 512):
        a[p, :8] = np.random.permutation(np.resize(levels, 8))
        for g in range(8):
            far = levels[np.abs(levels - a[p, g]) >= 10]
            a[p, g + 8] = far[np.random.randint(len(far))]
    return np.exp2(a.ravel()).repeat(32)


def f64(x):
    return np.asarray(x).astype(np.float64)


def striped(idx):
    return np.tile(idx.reshape(-1, 16).T, (8, 1)).astype(np.uint16)


def unstriped(offs):
    return offs[:16].T.reshape(-1).astype(np.int64)


E2M1 = np.array([0.0, 0.5, 1.0, 1.5, 2.0, 3.0, 4.0, 6.0, -0.0, -0.5, -1.0, -1.5, -2.0, -3.0, -4.0, -6.0])


def pack_weight(w, fmt):
    k, n = w.shape
    w = f64(np.asarray(w, np.float32).astype(ml_dtypes.bfloat16)).reshape(k // 32, 32, n)
    amax = np.abs(w).max(1)
    if fmt == "e4m3":
        byte = np.frexp(amax)[1] - 1 + 127 - 7
    else:
        mant, ex = np.frexp(amax / 6.0)
        byte = np.where(mant > 0.5, ex, ex - 1) + 127
    byte = np.clip(np.where(amax > 0, byte, 1), 1, 254)
    scaled = (w * np.exp2(127.0 - byte)[:, None, :]).reshape(k, n).astype(np.float32)
    by_word = np.ascontiguousarray(scaled.reshape(k // 512, 128, 4, n).transpose(0, 1, 3, 2))
    if fmt == "e4m3":
        words = by_word.astype(ml_dtypes.float8_e4m3fn).view(np.uint8)
    else:
        c = by_word.astype(ml_dtypes.float4_e2m1fn).view(np.uint8) & 0xF
        words = (c[..., 0::2] | (c[..., 1::2] << 4)).reshape(k // 512, 128, 2 * n)
    return np.ascontiguousarray(words), np.ascontiguousarray(byte.astype(np.uint8).reshape(k // 512, 16, n))


def unpack_weight(words, scales, fmt):
    g, _, n = scales.shape
    words = np.ascontiguousarray(words).reshape(g, 128, n, -1)
    if fmt == "e4m3":
        vals = words.view(ml_dtypes.float8_e4m3fn).astype(np.float64)
    else:
        nib = np.empty((g, 128, n, 4), np.uint8)
        nib[..., 0::2] = words & 0xF
        nib[..., 1::2] = words >> 4
        vals = E2M1[nib]
    vals = vals * np.repeat(np.exp2(scales.astype(np.float64) - 127.0), 8, axis=1)[..., None]
    return vals.transpose(0, 1, 3, 2).reshape(g * 512, n)


def gelu(v):
    return 0.5 * v * (1.0 + np.tanh(np.sqrt(2.0 / np.pi) * (v + 0.044715 * v**3)))


K, H, T, S, T2, P = 512, 1024, 4096, 1024, 2048, 512


def setup_inputs():
    n = np.random.standard_normal
    s = mx_kscale(K)[:, None]
    u = mx_kscale(H)[:, None]
    tab_words, tab_scales = pack_weight(n((K, T)) * s, "e4m3")
    wb_words, wb_scales = pack_weight(n((K, H)) / np.sqrt(K) / s, "e2m1")
    return {
        "tab_words": tab_words, "tab_scales": tab_scales,
        "offs": striped(np.random.permutation(T)[:S]),
        "wa": (n((K, H)) / np.sqrt(K) / s).astype(np.float32),
        "wb_words": wb_words, "wb_scales": wb_scales,
        "wc": (n((K, H)) / np.sqrt(K) / s).astype(np.float32),
        "gain": (1.2 * np.exp(0.3 * n(H)) * u[:, 0]).astype(np.float32),
        "page0": (n((H, T2)) * u).astype(np.float32),
        "wgs": np.exp(0.3 * n((128, S))).astype(np.float32),
        "offs2": striped(np.random.permutation(T2)[:S]),
        "offs3": striped(np.random.permutation(T2)[:P]),
        "offs4": striped(np.random.permutation(T2)[:P]),
        "base": (0.6 * n(H) * u[:, 0]).astype(np.float32),
        "wr": (n(H) / np.sqrt(H) / u[:, 0] ** 2).astype(np.float32),
        "bed": (0.8 * n(P)).astype(np.float32),
    }


def reference(tab_words, tab_scales, offs, wa, wb_words, wb_scales, wc, gain, page0, wgs,
              offs2, offs3, offs4, base, wr, bed):
    v = unpack_weight(tab_words, tab_scales, "e4m3")[:, unstriped(offs)]
    ya = mxq(f64(wa), 0, "e4m3").T @ v
    yb = unpack_weight(wb_words, wb_scales, "e2m1").T @ v
    yc = mxq(f64(wc), 0, "e4m3").T @ v
    h = np.tanh(np.maximum(ya, yb) + yc) * f64(gain)[:, None]
    page = f64(page0).copy()
    page[:, unstriped(offs2)] = np.tile(f64(wgs), (H // 128, 1)) * h
    x1 = page[:, unstriped(offs3)]
    x2 = (page[:, unstriped(offs4)] - f64(base)[:, None]) * f64(wr)[:, None]
    e = mxq(x1, 0, "e4m3").T @ mxq(x2, 0, "e4m3")
    return e + f64(bed)[:, None]

@@ -1,0 +1,355 @@
+from contextlib import ExitStack
+
+import concourse.mybir as mybir
+from concourse.masks import make_identity
+
+K, H, T, S, T2, NP = 512, 1024, 4096, 1024, 2048, 512
+FLOPS = 2 * (3 * K * H * S + H * NP * NP)
+
+F32 = mybir.dt.float32
+BF16 = mybir.dt.bfloat16
+I32 = mybir.dt.int32
+U32 = mybir.dt.uint32
+U16 = mybir.dt.uint16
+U8 = mybir.dt.uint8
+FP8X4 = mybir.dt.float8_e4m3fn_x4
+FP4X4 = mybir.dt.float4_e2m1fn_x4
+ALU = mybir.AluOpType
+ACT = mybir.ActivationFunctionType
+
+P = 128
+PACK = 4
+BANK = 512
+HALF = S // 2
+PASSES = H // (P * PACK)
+UNITS = HALF // P
+PHASES = 2 * PASSES
+RM, RA, RC = 4, 2, 2
+
+
+def tile_list_converter_fault_match_kernel(
+    tc, tab_words, tab_scales, offs, wa, wb_words, wb_scales, wc, gain, page0, wgs,
+    offs2, offs3, offs4, base, wr, bed, out,
+):
+    nc = tc.nc
+    with ExitStack() as ctx:
+        keep = ctx.enter_context(tc.tile_pool(name="keep", bufs=1))
+        pages = ctx.enter_context(tc.tile_pool(name="pages", bufs=6))
+        psum = ctx.enter_context(tc.psum_pool(name="psum", bufs=1))
+
+        def sbuf(name, shape, dtype):
+            return keep.tile(shape, dtype, name=name, align_bytes=64)
+
+        pick = keep.tile([P, S // 16], U16, name="pick")
+        put = keep.tile([P, S // 16], U16, name="put")
+        beds = keep.tile([P, NP // 16], U16, name="beds")
+        protos = keep.tile([P, NP // 16], U16, name="protos")
+        nc.sync.dma_start(pick[:], offs)
+
+        def load_rows(name, vec):
+            buf = sbuf(name, [P, PASSES, PACK], F32)
+            nc.sync.dma_start(buf[:], vec.rearrange("(b p t) -> p b t", p=P, t=PACK))
+            return buf
+
+
+        tab_s = sbuf("tab_s", [P, T], U8)
+        wb_s = sbuf("wb_s", [P, H], U8)
+
+        def load_plane(plane, src, clear, queue):
+            clear.memset(plane[:].bitcast(I32), 0)
+            for q in range(4):
+                queue.dma_start(
+                    plane[32 * q : 32 * q + 4, :].bitcast(I32), src[0, 4 * q : 4 * q + 4, :].bitcast(I32)
+                )
+        tab_w = sbuf("tab_w", [P, T], I32)
+        wb_w = sbuf("wb_w", [P, 2 * H], U8)
+
+        ident = sbuf("ident", [P, P], F32)
+        make_identity(nc, ident[:])
+
+        v_w = sbuf("v_w", [P, S], U32)
+        v_s = sbuf("v_s", [P, S], U8)
+
+        def gather_words(half):
+            nc.vector.tensor_copy(
+                v_s[:, half * HALF : (half + 1) * HALF], tab_s[:].indirect(pick[:, half * 32 : (half + 1) * 32])
+            )
+            nc.vector.tensor_copy(
+                v_w[:, half * HALF : (half + 1) * HALF],
+                tab_w[:].bitcast(U32).indirect(pick[:, half * 32 : (half + 1) * 32]),
+            )
+
+        raw = [sbuf(f"raw{i}", [P, PACK, BANK], F32) for i in range(2)]
+        x_woven = [sbuf(f"x_woven{i}", [P, NP, PACK], BF16) for i in range(2)]
+        pair = [sbuf(f"pair{i}", [P, 2 * BANK], F32) for i in range(2)]
+        woven = [buf[:].bitcast(BF16).rearrange("p (c t) -> p c t", t=PACK) for buf in pair]
+        w_codes = [sbuf(f"w_codes{i}", [P, H], U32) for i in range(2)]
+        w_planes = [sbuf(f"w_planes{i}", [P, H], U8) for i in range(2)]
+        weights = (wa, wc)
+
+        def weave(copy, dst, src):
+            copy(
+                dst.rearrange("p (c i) t -> p c t i", i=4),
+                src.rearrange("p t (c i) -> p c t i", i=4),
+            )
+
+        def load_weight(i, b):
+            cols = slice(b * BANK, (b + 1) * BANK)
+            nc.sync.dma_start(raw[i][:], weights[i].rearrange("(p t) r -> p t r", t=PACK)[:, :, cols])
+
+        def weave_weight(i, copy, lo, hi):
+            weave(copy, x_woven[i][:, lo:hi, :], raw[i][:, :, lo:hi])
+
+        def quantise_weight(i, b):
+            cols = slice(b * BANK, (b + 1) * BANK)
+            nc.vector.quantize_mx(
+                out=w_codes[i][:, cols].bitcast(FP8X4),
+                scales=w_planes[i][:, cols],
+                in_=x_woven[i][:].rearrange("p c t -> p (c t)"),
+            )
+
+        page = {}
+
+        def load_page(b, t):
+            buf = pages.tile([P, T2], F32, name="page")
+            nc.sync.dma_start(buf[:], page0.rearrange("(b p t) s -> b t p s", p=P, t=PACK)[b, t])
+            page[b, t] = buf
+
+        wgs_sb = {}
+
+        def load_wgs(lo, hi):
+            buf = sbuf(f"wgs_sb{lo}", [P, PACK, hi - lo], F32)
+            src = wgs.rearrange("(m t) j -> m t j", t=PACK)[:, :, lo:hi]
+            for q in range(4):
+                nc.sync.dma_start(buf[32 * q : 32 * (q + 1)], src)
+            wgs_sb[lo] = buf
+
+        ac_bank = [psum.tile([P, BANK], F32, name=f"ac_bank{i}") for i in range(UNITS)]
+        b_bank = [psum.tile([P, BANK], F32, name=f"b_bank{i}") for i in range(UNITS)]
+        a_sb = [sbuf(f"a_sb{i}", [P, BANK], F32) for i in range(RA)]
+        c_sb = [pair[i // 2][:, (i % 2) * BANK : (i % 2 + 1) * BANK] for i in range(UNITS)]
+        m_sb = [sbuf(f"m_sb{i}", [P, BANK], F32) for i in range(RM)]
+        w_sb = [sbuf(f"w_sb{i}", [P, BANK], F32) for i in range(3)]
+        h_sb = [sbuf(f"h_sb{i}", [P, PACK, HALF], F32) for i in range(2)]
+
+        def dealt(bank):
+            return bank[:].rearrange("j (m t) -> j t m", t=PACK)
+
+        def product(bank, phase, k, codes, plane):
+            half = phase % 2
+            tok = slice(half * HALF + k * P, half * HALF + (k + 1) * P)
+            nc.tensor.matmul_mx(
+                out=bank[:], lhsT=v_w[:, tok].bitcast(FP8X4), lhsT_scale=v_s[:, tok],
+                rhs=codes, rhs_scale=plane, start=True, stop=True,
+            )
+
+        def float_product(i, phase, k, dst, copy):
+            b = phase // 2
+            cols = slice(b * BANK, (b + 1) * BANK)
+            bank = ac_bank[2 * i + k % 2]
+            product(bank, phase, k, w_codes[i][:, cols].bitcast(FP8X4), w_planes[i][:, cols])
+            copy(dst, dealt(bank))
+
+        def packed_product(phase, k):
+            b = phase // 2
+            product(
+                b_bank[k], phase, k,
+                wb_w[:, 2 * b * BANK : 2 * (b + 1) * BANK].bitcast(FP4X4), wb_s[:, b * BANK : (b + 1) * BANK],
+            )
+
+        def by_slot(buf):
+            return buf[:].rearrange("j (t m) -> j t m", t=PACK)
+
+        def maximum(u):
+            nc.vector.tensor_tensor(by_slot(m_sb[u % RM]), dealt(b_bank[u % UNITS]), by_slot(a_sb[u % RA]), ALU.max)
+
+        def bend(u):
+            phase, k = divmod(u, UNITS)
+            z = b_bank[k][:].rearrange("p (t j) -> p t j", t=PACK)
+            for t in range(PACK):
+                nc.tensor.matmul(z[:, t, :], c_sb[2 * (u % RC) if RC == 2 else u % RC][:, t * P : (t + 1) * P], ident[:], start=True, stop=False, is_transpose=True)
+                nc.tensor.matmul(z[:, t, :], m_sb[u % RM][:, t * P : (t + 1) * P], ident[:], start=False, stop=True, is_transpose=True)
+            nc.scalar.activation(h_sb[phase % 2][:, :, k * P : (k + 1) * P], z, ACT.Tanh)
+
+        def larger(u):
+            packed_product(u // UNITS, u % UNITS)
+            float_product(0, u // UNITS, u % UNITS, by_slot(a_sb[u % RA]), nc.scalar.copy)
+            maximum(u)
+
+        def third(u, copy):
+            float_product(1, u // UNITS, u % UNITS, by_slot(c_sb[2 * (u % RC) if RC == 2 else u % RC]), copy)
+
+        def weigh(phase, t, lo, hi, factor):
+            b, half = divmod(phase, 2)
+            rows = wgs_sb[half * HALF + (lo if half == 0 and hi - lo < HALF else 0)][:, t, :]
+            if hi - lo == QUARTER:
+                nc.vector.tensor_scalar(factor, rows, gain_sb[:, b, t : t + 1], None, ALU.mult)
+            elif half == 0 and hi - lo == HALF:
+                for n in range(2):
+                    nc.scalar.activation(
+                        factor[:, n * QUARTER : (n + 1) * QUARTER], wgs_sb[n * QUARTER][:, t, :], ACT.Copy,
+                        scale=gain_sb[:, b, t : t + 1],
+                    )
+            else:
+                nc.scalar.activation(factor, rows, ACT.Copy, scale=gain_sb[:, b, t : t + 1])
+
+        def scatter(phase, t, lo, hi, factor):
+            b, half = divmod(phase, 2)
+            nc.vector.tensor_tensor(
+                page[b, t][:].indirect(put[:, (half * HALF + lo) // 16 : (half * HALF + hi) // 16]),
+                h_sb[phase % 2][:, t, lo:hi], factor, ALU.mult,
+            )
+
+        g1 = [sbuf("g1", [P, PACK, NP], F32), raw[0]]
+        g2 = [sbuf(f"g2_{i}", [P, NP], F32) for i in range(2)]
+        y2 = [sbuf(f"y2_{b}", [P, PACK, NP], BF16) for b in range(PASSES)]
+        x_codes = [[sbuf(f"x_codes{i}{b}", [P, NP], U32) for b in range(PASSES)] for i in range(2)]
+        x_planes = [[sbuf(f"x_planes{i}{b}", [P, NP], U8) for b in range(PASSES)] for i in range(2)]
+
+        def fetch(b, t):
+            direct = b == PASSES - 1 and t >= 2
+            nc.vector.tensor_copy(g2[t % 2][:], page[b, t][:].indirect(protos[:]))
+            nc.vector.tensor_copy(x_woven[0][:, :, t] if direct else g1[b][:, t, :], page[b, t][:].indirect(beds[:]))
+
+        def centre(b, t):
+            last = b == PASSES - 1 and t == PACK - 1
+            nc.scalar.activation(
+                x_woven[1][:, :, t] if last else y2[b][:, t, :], g2[t % 2][:], ACT.Identity,
+                bias=shift[:, b, t : t + 1], scale=wr_sb[:, b, t : t + 1],
+            )
+
+        def quantise_x(i, b, src):
+            nc.vector.quantize_mx(
+                out=x_codes[i][b][:].bitcast(FP8X4), scales=x_planes[i][b][:],
+                in_=src.rearrange("p c t -> p (c t)"),
+            )
+
+        def score(b, c):
+            rows = slice(c * P, (c + 1) * P)
+            nc.tensor.matmul_mx(
+                out=b_bank[c][:], lhsT=x_codes[0][b][:, rows].bitcast(FP8X4), lhsT_scale=x_planes[0][b][:, rows],
+                rhs=x_codes[1][b][:].bitcast(FP8X4), rhs_scale=x_planes[1][b][:],
+                start=(b == 0), stop=(b == PASSES - 1),
+            )
+
+        load_plane(wb_s, wb_scales, nc.gpsimd, nc.gpsimd)
+        load_weight(0, 0)
+        load_weight(1, 0)
+        nc.sync.dma_start(wb_w[:].bitcast(I32), wb_words[0].bitcast(I32))
+        nc.sync.dma_start(put[:], offs2)
+        load_plane(tab_s, tab_scales, nc.vector, nc.sync)
+        nc.sync.dma_start(tab_w[:], tab_words[0].rearrange("p t i -> p (t i)").bitcast(I32))
+        gain_sb = load_rows("gain_sb", gain)
+        QUARTER = HALF // 2
+        load_page(0, 0)
+        load_wgs(0, QUARTER)
+        load_page(0, 1)
+        load_wgs(QUARTER, HALF)
+        for i in range(2):
+            weave_weight(i, nc.vector.tensor_copy, 0, BANK // 2)
+            weave_weight(i, nc.scalar.copy, BANK // 2, BANK)
+            quantise_weight(i, 0)
+        gather_words(0)
+        larger(0)
+        third(0, nc.scalar.copy)
+        larger(1)
+        nc.sync.dma_start(beds[:], offs3)
+        nc.sync.dma_start(protos[:], offs4)
+        load_page(0, 2)
+        load_page(0, 3)
+        load_wgs(HALF, S)
+        load_weight(0, 1)
+        load_weight(1, 1)
+        base_sb = load_rows("base_sb", base)
+        wr_sb = load_rows("wr_sb", wr)
+        third(1, nc.vector.tensor_copy)
+        bend(0)
+        bend(1)
+        gather_words(1)
+        shift = sbuf("shift", [P, PASSES, PACK], F32)
+        nc.vector.scalar_tensor_tensor(shift[:], base_sb[:], -1.0, wr_sb[:], ALU.mult, ALU.mult)
+
+        larger(2)
+        third(2, nc.scalar.copy)
+        PLAN = {i: [("l", i + 3), ("t", i + 3), ("b", i + 2)] for i in range(5)}
+        PLAN[5] = [("b", 7)]
+        PLAN[8] = [("l", 8), ("l", 9), ("l", 10), ("l", 11), ("t", 8), ("t", 9)]
+        PLAN[9] = [("b", 8), ("t", 10), ("b", 9), ("t", 11)]
+        PLAN[10] = [("b", 10), ("l", 12), ("t", 12), ("b", 11)]
+        PLAN = dict(list(PLAN.items()) + list({i: [("l", i + 2), ("t", i + 2), ("b", i + 1)] for i in range(11, 14)}.items()))
+        PLAN[14] = [("b", 15)]
+        steps = [(0, t, lo, lo + QUARTER) for lo in (0, QUARTER) for t in range(2)]
+        steps = steps + [(0, t, 0, HALF) for t in range(2, PACK)]
+        steps = steps + [(phase, t, 0, HALF) for phase in range(1, PHASES) for t in range(PACK)]
+        for i, (phase, t, lo, hi) in enumerate(steps):
+            b, half = divmod(phase, 2)
+            if i in (4, 5, 6):
+                factor = w_sb[i % 3][:]
+                weigh(phase, t, lo, hi, factor)
+            if i in (7, 8):
+                weave_weight(i - 7, nc.scalar.copy, 0, BANK)
+                quantise_weight(i - 7, 1)
+            for kind, u in PLAN.get(i, ()):
+                if kind == "l":
+                    larger(u)
+                elif kind == "t":
+                    third(u, nc.scalar.copy)
+                else:
+                    bend(u)
+            if phase == 1:
+                load_page(1, t)
+            if i < 4:
+                factor = m_sb[i][:, 0 : hi - lo]
+            elif i < 7:
+                pass
+            elif i < 9:
+                factor = raw[i - 7][:, 0, :]
+            elif i == 9:
+                factor = m_sb[1][:]
+            elif i < 15:
+                factor = m_sb[(i + 1) % RM][:]
+            elif i == 16:
+                factor = y2[0][:, 0:2, :].rearrange("p t c -> p (t c)").bitcast(F32)
+            elif i == 17:
+                fetch(b, 2)
+                centre(b, 2)
+                factor = g2[0][:]
+            else:
+                factor = w_sb[i % 2][:]
+            if i not in (4, 5, 6):
+                weigh(phase, t, lo, hi, factor)
+            if i in (8, 9, 10, 11):
+                centre(0, i - 8)
+            if i == 16:
+                centre(1, 0)
+            scatter(phase, t, lo, hi, factor)
+            if i in (7, 8, 9, 10):
+                fetch(0, i - 7)
+            if i in (15, 16):
+                fetch(1, i - 15)
+            if i == 15:
+                for n, src in enumerate((g1[0], y2[0])):
+                    weave(nc.scalar.copy, woven[n], src[:])
+                    quantise_x(n, 0, woven[n])
+                for c in range(UNITS):
+                    score(0, c)
+            if i == 16:
+                centre(1, 1)
+                nc.scalar.copy(x_woven[0][:, :, 0:2], g1[1][:, 0:2, :].rearrange("p t c -> p c t"))
+        nc.scalar.copy(x_woven[1][:, :, 0:3], y2[1][:, 0:3, :].rearrange("p t c -> p c t"))
+        fetch(1, 3)
+        centre(1, 3)
+
+        bed_sb = sbuf("bed_sb", [P, UNITS], F32)
+        with nc.allow_non_contiguous_dma(reason="one offset for each output row"):
+            nc.sync.dma_start(bed_sb[:], bed.rearrange("(c p) -> p c", p=P))
+        quantise_x(1, 1, x_woven[1][:])
+        quantise_x(0, 1, x_woven[0][:])
+        for c in range(UNITS):
+            score(1, c)
+            res = sbuf(f"res{c}", [P, NP], F32)
+            if c % 2 == 0:
+                nc.scalar.activation(res[:], b_bank[c][:], ACT.Identity, bias=bed_sb[:, c : c + 1])
+            else:
+                nc.vector.tensor_scalar(res[:], b_bank[c][:], bed_sb[:, c : c + 1], None, ALU.add)
+            nc.sync.dma_start(out[c * P : (c + 1) * P, :], res[:])

@@ -98,7 +98,13 @@ def tile_list_converter_fault_match_kernel(
             nc.sync.dma_start(raw[i][:], weights[i].rearrange("(p t) r -> p t r", t=PACK)[:, :, cols])
 
         def weave_weight(i, copy, lo, hi):
-            weave(copy, x_woven[i][:, lo:hi, :], raw[i][:, :, lo:hi])
+            if i == 0:
+                dst = x_woven[i][:].rearrange("p (u m e) j -> p m j u e", u=2, e=2)
+                src = raw[i][:].rearrange("p j (m u e) -> p m j u e", u=2, e=2)
+            else:
+                dst = x_woven[i][:].rearrange("p (t m) j -> p m j t", t=PACK)
+                src = raw[i][:].rearrange("p j (m t) -> p m j t", t=PACK)
+            copy(dst[:, lo // PACK : hi // PACK], src[:, lo // PACK : hi // PACK])
 
         def quantise_weight(i, b):
             cols = slice(b * BANK, (b + 1) * BANK)
@@ -132,8 +138,6 @@ def tile_list_converter_fault_match_kernel(
         w_sb = [sbuf(f"w_sb{i}", [P, BANK], F32) for i in range(3)]
         h_sb = [sbuf(f"h_sb{i}", [P, PACK, HALF], F32) for i in range(2)]
 
-        def dealt(bank):
-            return bank[:].rearrange("j (m t) -> j t m", t=PACK)
 
         def product(bank, phase, k, codes, plane):
             half = phase % 2
@@ -148,7 +152,7 @@ def tile_list_converter_fault_match_kernel(
             cols = slice(b * BANK, (b + 1) * BANK)
             bank = ac_bank[2 * i + k % 2]
             product(bank, phase, k, w_codes[i][:, cols].bitcast(FP8X4), w_planes[i][:, cols])
-            copy(dst, dealt(bank))
+            copy(dst, bank[:])
 
         def packed_product(phase, k):
             b = phase // 2
@@ -157,27 +161,28 @@ def tile_list_converter_fault_match_kernel(
                 wb_w[:, 2 * b * BANK : 2 * (b + 1) * BANK].bitcast(FP4X4), wb_s[:, b * BANK : (b + 1) * BANK],
             )
 
-        def by_slot(buf):
-            return buf[:].rearrange("j (t m) -> j t m", t=PACK)
+        def by_pair(buf):
+            return buf[:].rearrange("j (u m e) -> j u m e", u=2, e=2)
 
         def maximum(u):
-            nc.vector.tensor_tensor(by_slot(m_sb[u % RM]), dealt(b_bank[u % UNITS]), by_slot(a_sb[u % RA]), ALU.max)
+            natural = b_bank[u % UNITS][:].rearrange("j (m u e) -> j u m e", u=2, e=2)
+            nc.vector.tensor_tensor(by_pair(m_sb[u % RM]), natural, by_pair(a_sb[u % RA]), ALU.max)
 
         def bend(u):
             phase, k = divmod(u, UNITS)
             z = b_bank[k][:].rearrange("p (t j) -> p t j", t=PACK)
             for t in range(PACK):
-                nc.tensor.matmul(z[:, t, :], c_sb[2 * (u % RC) if RC == 2 else u % RC][:, t * P : (t + 1) * P], ident[:], start=True, stop=False, is_transpose=True)
-                nc.tensor.matmul(z[:, t, :], m_sb[u % RM][:, t * P : (t + 1) * P], ident[:], start=False, stop=True, is_transpose=True)
+                nc.tensor.matmul(z[:, t, :], c_sb[2 * (u % RC)][:, t * P : (t + 1) * P], ident[:], start=True, stop=False, is_transpose=True)
+                nc.tensor.matmul(z[:, t, :], by_pair(m_sb[u % RM])[:, t // 2, :, t % 2], ident[:], start=False, stop=True, is_transpose=True)
             nc.scalar.activation(h_sb[phase % 2][:, :, k * P : (k + 1) * P], z, ACT.Tanh)
 
         def larger(u):
             packed_product(u // UNITS, u % UNITS)
-            float_product(0, u // UNITS, u % UNITS, by_slot(a_sb[u % RA]), nc.scalar.copy)
+            float_product(0, u // UNITS, u % UNITS, a_sb[u % RA][:], nc.scalar.copy)
             maximum(u)
 
         def third(u, copy):
-            float_product(1, u // UNITS, u % UNITS, by_slot(c_sb[2 * (u % RC) if RC == 2 else u % RC]), copy)
+            float_product(1, u // UNITS, u % UNITS, c_sb[2 * (u % RC)], copy)
 
         def weigh(phase, t, lo, hi, factor):
             b, half = divmod(phase, 2)
@@ -337,14 +342,24 @@ def tile_list_converter_fault_match_kernel(
                 centre(1, 1)
                 nc.scalar.copy(x_woven[0][:, :, 0:2], g1[1][:, 0:2, :].rearrange("p t c -> p c t"))
         nc.scalar.copy(x_woven[1][:, :, 0:3], y2[1][:, 0:3, :].rearrange("p t c -> p c t"))
-        fetch(1, 3)
-        centre(1, 3)
+        for n in range(2):
+            cols = slice(n * QUARTER, (n + 1) * QUARTER)
+            nc.vector.tensor_copy(g2[1][:, cols], page[1, 3][:].indirect(protos[:, 16 * n : 16 * (n + 1)]))
+            nc.scalar.activation(
+                x_woven[1][:, cols, 3], g2[1][:, cols], ACT.Identity, bias=shift[:, 1, 3:4], scale=wr_sb[:, 1, 3:4]
+            )
+        nc.vector.tensor_copy(x_woven[0][:, :, 3], page[1, 3][:].indirect(beds[:]))
 
         bed_sb = sbuf("bed_sb", [P, UNITS], F32)
         with nc.allow_non_contiguous_dma(reason="one offset for each output row"):
             nc.sync.dma_start(bed_sb[:], bed.rearrange("(c p) -> p c", p=P))
         quantise_x(1, 1, x_woven[1][:])
-        quantise_x(0, 1, x_woven[0][:])
+        for n in range(2):
+            cols = slice(n * QUARTER, (n + 1) * QUARTER)
+            nc.vector.quantize_mx(
+                out=x_codes[0][1][:, cols].bitcast(FP8X4), scales=x_planes[0][1][:, cols],
+                in_=x_woven[0][:, cols, :].rearrange("p c t -> p (c t)"),
+            )
         for c in range(UNITS):
             score(1, c)
             res = sbuf(f"res{c}", [P, NP], F32)

@@ -24,7 +24,9 @@ HALF = S // 2
 PASSES = H // (P * PACK)
 UNITS = HALF // P
 PHASES = 2 * PASSES
-RM, RA, RC = 4, 2, 2
+CS = 11
+RM, RA, RC = 4, 3, 2
+FREE = {0: 0, 4: 1, 5: 2, 6: 0, 15: 1, 16: 2}
 
 
 def tile_list_converter_fault_match_kernel(
@@ -37,8 +39,8 @@ def tile_list_converter_fault_match_kernel(
         pages = ctx.enter_context(tc.tile_pool(name="pages", bufs=6))
         psum = ctx.enter_context(tc.psum_pool(name="psum", bufs=1))
 
-        def sbuf(name, shape, dtype):
-            return keep.tile(shape, dtype, name=name, align_bytes=64)
+        def sbuf(name, shape, dtype, tag=None):
+            return keep.tile(shape, dtype, name=name, tag=tag or name, align_bytes=64)
 
         pick = keep.tile([P, S // 16], U16, name="pick")
         put = keep.tile([P, S // 16], U16, name="put")
@@ -121,14 +123,13 @@ def tile_list_converter_fault_match_kernel(
             nc.sync.dma_start(buf[:], page0.rearrange("(b p t) s -> b t p s", p=P, t=PACK)[b, t])
             page[b, t] = buf
 
-        wgs_sb = {}
+        wgs_sb = [sbuf(f"wgs_sb{half}", [P, PACK, HALF], F32) for half in range(2)]
 
         def load_wgs(lo, hi):
-            buf = sbuf(f"wgs_sb{lo}", [P, PACK, hi - lo], F32)
+            half, first = divmod(lo, HALF)
             src = wgs.rearrange("(m t) j -> m t j", t=PACK)[:, :, lo:hi]
-            for q in range(4):
-                nc.sync.dma_start(buf[32 * q : 32 * (q + 1)], src)
-            wgs_sb[lo] = buf
+            for q in (0, 2, 1, 3):
+                nc.sync.dma_start(wgs_sb[half][32 * q : 32 * (q + 1), :, first : first + hi - lo], src)
 
         ac_bank = [psum.tile([P, BANK], F32, name=f"ac_bank{i}") for i in range(UNITS)]
         b_bank = [psum.tile([P, BANK], F32, name=f"b_bank{i}") for i in range(UNITS)]
@@ -170,10 +171,17 @@ def tile_list_converter_fault_match_kernel(
 
         def bend(u):
             phase, k = divmod(u, UNITS)
-            z = b_bank[k][:].rearrange("p (t j) -> p t j", t=PACK)
+            z = ac_bank[2 + k % 2][:].rearrange("p (t j) -> p t j", t=PACK)
             for t in range(PACK):
-                nc.tensor.matmul(z[:, t, :], c_sb[2 * (u % RC)][:, t * P : (t + 1) * P], ident[:], start=True, stop=False, is_transpose=True)
-                nc.tensor.matmul(z[:, t, :], by_pair(m_sb[u % RM])[:, t // 2, :, t % 2], ident[:], start=False, stop=True, is_transpose=True)
+                nc.tensor.matmul(
+                    z[:, t, :], c_sb[u % UNITS][:, t * P : (t + 1) * P], ident[:],
+                    start=(t == 0), stop=False, is_transpose=True,
+                )
+            for t in range(PACK):
+                nc.tensor.matmul(
+                    z[:, t, :], by_pair(m_sb[u % RM])[:, t // 2, :, t % 2], ident[:],
+                    start=False, stop=(t == PACK - 1), is_transpose=True,
+                )
             nc.scalar.activation(h_sb[phase % 2][:, :, k * P : (k + 1) * P], z, ACT.Tanh)
 
         def larger(u):
@@ -182,19 +190,13 @@ def tile_list_converter_fault_match_kernel(
             maximum(u)
 
         def third(u, copy):
-            float_product(1, u // UNITS, u % UNITS, c_sb[2 * (u % RC)], copy)
+            float_product(1, u // UNITS, u % UNITS, c_sb[u % UNITS], copy)
 
         def weigh(phase, t, lo, hi, factor):
             b, half = divmod(phase, 2)
-            rows = wgs_sb[half * HALF + (lo if half == 0 and hi - lo < HALF else 0)][:, t, :]
-            if hi - lo == QUARTER:
+            rows = wgs_sb[half][:, t, lo:hi]
+            if hi - lo == QUARTER or (phase, t) == (1, 0):
                 nc.vector.tensor_scalar(factor, rows, gain_sb[:, b, t : t + 1], None, ALU.mult)
-            elif half == 0 and hi - lo == HALF:
-                for n in range(2):
-                    nc.scalar.activation(
-                        factor[:, n * QUARTER : (n + 1) * QUARTER], wgs_sb[n * QUARTER][:, t, :], ACT.Copy,
-                        scale=gain_sb[:, b, t : t + 1],
-                    )
             else:
                 nc.scalar.activation(factor, rows, ACT.Copy, scale=gain_sb[:, b, t : t + 1])
 
@@ -206,20 +208,22 @@ def tile_list_converter_fault_match_kernel(
             )
 
         g1 = [sbuf("g1", [P, PACK, NP], F32), raw[0]]
-        g2 = [sbuf(f"g2_{i}", [P, NP], F32) for i in range(2)]
-        y2 = [sbuf(f"y2_{b}", [P, PACK, NP], BF16) for b in range(PASSES)]
-        x_codes = [[sbuf(f"x_codes{i}{b}", [P, NP], U32) for b in range(PASSES)] for i in range(2)]
+        g2 = [sbuf(f"g2_{i}", [P, NP], F32) for i in range(PACK)]
+        y2 = [sbuf("y2_0", [P, PACK, NP], BF16, "late"), sbuf("y2_1", [P, PACK, NP], BF16)]
+        x_codes = [[sbuf(f"x_codes0{b}", [P, NP], U32) for b in range(PASSES)]]
+        last_factor = sbuf("last_factor", [P, HALF], F32, "late")
+        x_codes.append([sbuf("x_codes10", [P, NP], U32, "late"), sbuf("x_codes11", [P, NP], U32)])
         x_planes = [[sbuf(f"x_planes{i}{b}", [P, NP], U8) for b in range(PASSES)] for i in range(2)]
 
         def fetch(b, t):
             direct = b == PASSES - 1 and t >= 2
-            nc.vector.tensor_copy(g2[t % 2][:], page[b, t][:].indirect(protos[:]))
+            nc.vector.tensor_copy(g2[t][:], page[b, t][:].indirect(protos[:]))
             nc.vector.tensor_copy(x_woven[0][:, :, t] if direct else g1[b][:, t, :], page[b, t][:].indirect(beds[:]))
 
         def centre(b, t):
             last = b == PASSES - 1 and t == PACK - 1
             nc.scalar.activation(
-                x_woven[1][:, :, t] if last else y2[b][:, t, :], g2[t % 2][:], ACT.Identity,
+                x_woven[1][:, :, t] if last else y2[b][:, t, :], g2[t][:], ACT.Identity,
                 bias=shift[:, b, t : t + 1], scale=wr_sb[:, b, t : t + 1],
             )
 
@@ -274,22 +278,34 @@ def tile_list_converter_fault_match_kernel(
         shift = sbuf("shift", [P, PASSES, PACK], F32)
         nc.vector.scalar_tensor_tensor(shift[:], base_sb[:], -1.0, wr_sb[:], ALU.mult, ALU.mult)
 
-        larger(2)
-        third(2, nc.scalar.copy)
-        PLAN = {i: [("l", i + 3), ("t", i + 3), ("b", i + 2)] for i in range(5)}
-        PLAN[5] = [("b", 7)]
+        PLAN = {0: [("l", 2), ("t", 2), ("l", 3), ("b", 2)], 1: [("t", 3), ("b", 3)]}
+        for i in range(2, 6):
+            PLAN[i] = [("l", i + 2), ("t", i + 2), ("b", i + 2)]
         PLAN[8] = [("l", 8), ("l", 9), ("l", 10), ("l", 11), ("t", 8), ("t", 9)]
-        PLAN[9] = [("b", 8), ("t", 10), ("b", 9), ("t", 11)]
-        PLAN[10] = [("b", 10), ("l", 12), ("t", 12), ("b", 11)]
-        PLAN = dict(list(PLAN.items()) + list({i: [("l", i + 2), ("t", i + 2), ("b", i + 1)] for i in range(11, 14)}.items()))
-        PLAN[14] = [("b", 15)]
+        PLAN[9] = [("b", 8), ("w", 0), ("t", 10), ("b", 9), ("t", 11), ("l", 12)]
+        PLAN[10] = [("b", 10), ("t", 12), ("b", 11), ("w", 0), ("l", 13), ("t", 13), ("b", 12)]
+        for i in range(11, 13):
+            PLAN[i] = [("l", i + 3), ("t", i + 3), ("b", i + 2)]
+        PLAN[13] = [("b", 15)]
         steps = [(0, t, lo, lo + QUARTER) for lo in (0, QUARTER) for t in range(2)]
         steps = steps + [(0, t, 0, HALF) for t in range(2, PACK)]
         steps = steps + [(phase, t, 0, HALF) for phase in range(1, PHASES) for t in range(PACK)]
         for i, (phase, t, lo, hi) in enumerate(steps):
             b, half = divmod(phase, 2)
-            if i in (4, 5, 6):
-                factor = w_sb[i % 3][:]
+            if 1 <= i <= 4:
+                factor = m_sb[i - 1][:, 0 : hi - lo]
+            elif i in (7, 8):
+                factor = raw[i - 7][:, 0, :]
+            elif i == 9:
+                factor = c_sb[0]
+            elif 10 <= i <= 14:
+                factor = m_sb[(i + 1) % RM][:]
+            elif i == 17:
+                factor = last_factor[:]
+            else:
+                factor = w_sb[FREE[i]][:, 0 : hi - lo]
+            early = i in (0, 1, 2, 3, 4, 5, 6, 11, 12, 13, 14)
+            if early:
                 weigh(phase, t, lo, hi, factor)
             if i in (7, 8):
                 weave_weight(i - 7, nc.scalar.copy, 0, BANK)
@@ -299,55 +315,42 @@ def tile_list_converter_fault_match_kernel(
                     larger(u)
                 elif kind == "t":
                     third(u, nc.scalar.copy)
+                elif kind == "w":
+                    weigh(phase, t, lo, hi, factor)
                 else:
                     bend(u)
             if phase == 1:
                 load_page(1, t)
-            if i < 4:
-                factor = m_sb[i][:, 0 : hi - lo]
-            elif i < 7:
-                pass
-            elif i < 9:
-                factor = raw[i - 7][:, 0, :]
-            elif i == 9:
-                factor = m_sb[1][:]
-            elif i < 15:
-                factor = m_sb[(i + 1) % RM][:]
-            elif i == 16:
-                factor = y2[0][:, 0:2, :].rearrange("p t c -> p (t c)").bitcast(F32)
-            elif i == 17:
-                fetch(b, 2)
-                centre(b, 2)
-                factor = g2[0][:]
-            else:
-                factor = w_sb[i % 2][:]
-            if i not in (4, 5, 6):
+            if i == 15:
+                for n, src in enumerate((g1[0], y2[0])):
+                    weave(nc.scalar.copy, woven[n], src[:])
+                quantise_x(0, 0, woven[0])
+                weigh(3, 3, 0, HALF, last_factor[:])
+            if not early and i not in (9, 10, 17):
                 weigh(phase, t, lo, hi, factor)
-            if i in (8, 9, 10, 11):
-                centre(0, i - 8)
-            if i == 16:
-                centre(1, 0)
+            if i in (CS, CS + 1, CS + 2, CS + 3):
+                centre(0, i - CS)
+            if i in (16, 17):
+                centre(1, i - 16)
+            if i == 17:
+                fetch(1, 2)
+                centre(1, 2)
+                nc.scalar.copy(x_woven[0][:, :, 0:2], g1[1][:, 0:2, :].rearrange("p t c -> p c t"))
+                nc.scalar.copy(x_woven[1][:, :, 0:3], y2[1][:, 0:3, :].rearrange("p t c -> p c t"))
             scatter(phase, t, lo, hi, factor)
             if i in (7, 8, 9, 10):
                 fetch(0, i - 7)
             if i in (15, 16):
                 fetch(1, i - 15)
-            if i == 15:
-                for n, src in enumerate((g1[0], y2[0])):
-                    weave(nc.scalar.copy, woven[n], src[:])
-                    quantise_x(n, 0, woven[n])
-                for c in range(UNITS):
-                    score(0, c)
-            if i == 16:
-                centre(1, 1)
-                nc.scalar.copy(x_woven[0][:, :, 0:2], g1[1][:, 0:2, :].rearrange("p t c -> p c t"))
-        nc.scalar.copy(x_woven[1][:, :, 0:3], y2[1][:, 0:3, :].rearrange("p t c -> p c t"))
         for n in range(2):
             cols = slice(n * QUARTER, (n + 1) * QUARTER)
-            nc.vector.tensor_copy(g2[1][:, cols], page[1, 3][:].indirect(protos[:, 16 * n : 16 * (n + 1)]))
+            nc.vector.tensor_copy(g2[3][:, cols], page[1, 3][:].indirect(protos[:, 16 * n : 16 * (n + 1)]))
             nc.scalar.activation(
-                x_woven[1][:, cols, 3], g2[1][:, cols], ACT.Identity, bias=shift[:, 1, 3:4], scale=wr_sb[:, 1, 3:4]
+                x_woven[1][:, cols, 3], g2[3][:, cols], ACT.Identity, bias=shift[:, 1, 3:4], scale=wr_sb[:, 1, 3:4]
             )
+        quantise_x(1, 0, woven[1])
+        for c in range(UNITS):
+            score(0, c)
         nc.vector.tensor_copy(x_woven[0][:, :, 3], page[1, 3][:].indirect(beds[:]))
 
         bed_sb = sbuf("bed_sb", [P, UNITS], F32)

@@ -20,13 +20,14 @@ ACT = mybir.ActivationFunctionType
 P = 128
 PACK = 4
 BANK = 512
+GROUP = 16
 HALF = S // 2
-PASSES = H // (P * PACK)
+QUARTER = S // 4
+PASSES = H // BANK
 UNITS = HALF // P
-PHASES = 2 * PASSES
-CS = 11
-RM, RA, RC = 4, 3, 2
-FREE = {0: 0, 4: 1, 5: 2, 6: 0, 15: 1, 16: 2}
+PAGE_BUFS = 6
+A_BUFS = 3
+WARM_PASSES = 3
 
 
 def tile_list_converter_fault_match_kernel(
@@ -36,94 +37,76 @@ def tile_list_converter_fault_match_kernel(
     nc = tc.nc
     with ExitStack() as ctx:
         keep = ctx.enter_context(tc.tile_pool(name="keep", bufs=1))
-        pages = ctx.enter_context(tc.tile_pool(name="pages", bufs=6))
+        pages = ctx.enter_context(tc.tile_pool(name="pages", bufs=PAGE_BUFS))
         psum = ctx.enter_context(tc.psum_pool(name="psum", bufs=1))
 
         def sbuf(name, shape, dtype, tag=None):
             return keep.tile(shape, dtype, name=name, tag=tag or name, align_bytes=64)
 
-        pick = keep.tile([P, S // 16], U16, name="pick")
-        put = keep.tile([P, S // 16], U16, name="put")
-        beds = keep.tile([P, NP // 16], U16, name="beds")
-        protos = keep.tile([P, NP // 16], U16, name="protos")
-        nc.sync.dma_start(pick[:], offs)
+        def entries(offsets, lo, hi):
+            return offsets[:, lo // GROUP : hi // GROUP]
 
-        def load_rows(name, vec):
+        pick = keep.tile([P, S // GROUP], U16, name="pick")
+        put = keep.tile([P, S // GROUP], U16, name="put")
+        beds = keep.tile([P, NP // GROUP], U16, name="beds")
+        protos = keep.tile([P, NP // GROUP], U16, name="protos")
+
+        tab_w = sbuf("tab_w", [P, T], I32)
+        tab_s = sbuf("tab_s", [P, T], U8)
+        wb_w = sbuf("wb_w", [P, 2 * H], U8)
+        wb_s = sbuf("wb_s", [P, H], U8)
+        v_w = sbuf("v_w", [P, S], U32)
+        v_s = sbuf("v_s", [P, S], U8)
+        ident = sbuf("ident", [P, P], F32)
+
+        weights = (wa, wc)
+        raw = [sbuf(f"raw{i}", [P, PACK, BANK], F32) for i in range(2)]
+        w_codes = [sbuf(f"w_codes{i}", [P, H], U32) for i in range(2)]
+        w_scales = [sbuf(f"w_scales{i}", [P, H], U8) for i in range(2)]
+        woven = [sbuf(f"woven{i}", [P, BANK, PACK], BF16) for i in range(2)]
+
+        a_bank = [psum.tile([P, BANK], F32, name=f"a_bank{i}") for i in range(2)]
+        c_bank = [psum.tile([P, BANK], F32, name=f"c_bank{i}") for i in range(2)]
+        b_bank = [psum.tile([P, BANK], F32, name=f"b_bank{i}") for i in range(UNITS)]
+        a_sb = [sbuf(f"a_sb{i}", [P, BANK], F32) for i in range(A_BUFS)]
+        m_sb = [sbuf(f"m_sb{i}", [P, BANK], F32) for i in range(UNITS)]
+        c_pair = [sbuf(f"c_pair{i}", [P, 2 * BANK], F32) for i in range(2)]
+        c_sb = [c_pair[k // 2][:, (k % 2) * BANK : (k % 2 + 1) * BANK] for k in range(UNITS)]
+        h_sb = [sbuf(f"h_sb{half}", [P, PACK, HALF], F32) for half in range(2)]
+        wgs_sb = [sbuf(f"wgs_sb{half}", [P, PACK, HALF], F32) for half in range(2)]
+        spare = [sbuf(f"spare{i}", [P, HALF], F32) for i in range(3)]
+        page = {}
+
+        x1_rows = [sbuf("x1_rows0", [P, PACK, NP], F32), raw[0]]
+        x2_picked = [sbuf(f"x2_picked{t}", [P, NP], F32) for t in range(PACK)]
+        x2_rows = [sbuf("x2_rows0", [P, PACK, NP], BF16, "late"), sbuf("x2_rows1", [P, PACK - 1, NP], BF16)]
+        last_factor = sbuf("last_factor", [P, HALF], F32, "late")
+        x_codes = [
+            [sbuf(f"x1_codes{b}", [P, NP], U32) for b in range(PASSES)],
+            [sbuf("x2_codes0", [P, NP], U32, "late"), sbuf("x2_codes1", [P, NP], U32)],
+        ]
+        x_scales = [[sbuf(f"x{i + 1}_scales{b}", [P, NP], U8) for b in range(PASSES)] for i in range(2)]
+
+        def load_scales(plane, src, clearing_engine):
+            clearing_engine.memset(plane[:].bitcast(I32), 0)
+            for q in range(4):
+                nc.sync.dma_start(
+                    plane[32 * q : 32 * q + 4, :].bitcast(I32), src[0, 4 * q : 4 * q + 4, :].bitcast(I32)
+                )
+
+        def load_weight(i, b):
+            rows = weights[i].rearrange("(p t) r -> p t r", t=PACK)
+            nc.sync.dma_start(raw[i][:], rows[:, :, b * BANK : (b + 1) * BANK])
+
+        def load_by_row(name, vec):
             buf = sbuf(name, [P, PASSES, PACK], F32)
             nc.sync.dma_start(buf[:], vec.rearrange("(b p t) -> p b t", p=P, t=PACK))
             return buf
-
-
-        tab_s = sbuf("tab_s", [P, T], U8)
-        wb_s = sbuf("wb_s", [P, H], U8)
-
-        def load_plane(plane, src, clear, queue):
-            clear.memset(plane[:].bitcast(I32), 0)
-            for q in range(4):
-                queue.dma_start(
-                    plane[32 * q : 32 * q + 4, :].bitcast(I32), src[0, 4 * q : 4 * q + 4, :].bitcast(I32)
-                )
-        tab_w = sbuf("tab_w", [P, T], I32)
-        wb_w = sbuf("wb_w", [P, 2 * H], U8)
-
-        ident = sbuf("ident", [P, P], F32)
-        make_identity(nc, ident[:])
-
-        v_w = sbuf("v_w", [P, S], U32)
-        v_s = sbuf("v_s", [P, S], U8)
-
-        def gather_words(half):
-            nc.vector.tensor_copy(
-                v_s[:, half * HALF : (half + 1) * HALF], tab_s[:].indirect(pick[:, half * 32 : (half + 1) * 32])
-            )
-            nc.vector.tensor_copy(
-                v_w[:, half * HALF : (half + 1) * HALF],
-                tab_w[:].bitcast(U32).indirect(pick[:, half * 32 : (half + 1) * 32]),
-            )
-
-        raw = [sbuf(f"raw{i}", [P, PACK, BANK], F32) for i in range(2)]
-        x_woven = [sbuf(f"x_woven{i}", [P, NP, PACK], BF16) for i in range(2)]
-        pair = [sbuf(f"pair{i}", [P, 2 * BANK], F32) for i in range(2)]
-        woven = [buf[:].bitcast(BF16).rearrange("p (c t) -> p c t", t=PACK) for buf in pair]
-        w_codes = [sbuf(f"w_codes{i}", [P, H], U32) for i in range(2)]
-        w_planes = [sbuf(f"w_planes{i}", [P, H], U8) for i in range(2)]
-        weights = (wa, wc)
-
-        def weave(copy, dst, src):
-            copy(
-                dst.rearrange("p (c i) t -> p c t i", i=4),
-                src.rearrange("p t (c i) -> p c t i", i=4),
-            )
-
-        def load_weight(i, b):
-            cols = slice(b * BANK, (b + 1) * BANK)
-            nc.sync.dma_start(raw[i][:], weights[i].rearrange("(p t) r -> p t r", t=PACK)[:, :, cols])
-
-        def weave_weight(i, copy, lo, hi):
-            if i == 0:
-                dst = x_woven[i][:].rearrange("p (u m e) j -> p m j u e", u=2, e=2)
-                src = raw[i][:].rearrange("p j (m u e) -> p m j u e", u=2, e=2)
-            else:
-                dst = x_woven[i][:].rearrange("p (t m) j -> p m j t", t=PACK)
-                src = raw[i][:].rearrange("p j (m t) -> p m j t", t=PACK)
-            copy(dst[:, lo // PACK : hi // PACK], src[:, lo // PACK : hi // PACK])
-
-        def quantise_weight(i, b):
-            cols = slice(b * BANK, (b + 1) * BANK)
-            nc.vector.quantize_mx(
-                out=w_codes[i][:, cols].bitcast(FP8X4),
-                scales=w_planes[i][:, cols],
-                in_=x_woven[i][:].rearrange("p c t -> p (c t)"),
-            )
-
-        page = {}
 
         def load_page(b, t):
             buf = pages.tile([P, T2], F32, name="page")
             nc.sync.dma_start(buf[:], page0.rearrange("(b p t) s -> b t p s", p=P, t=PACK)[b, t])
             page[b, t] = buf
-
-        wgs_sb = [sbuf(f"wgs_sb{half}", [P, PACK, HALF], F32) for half in range(2)]
 
         def load_wgs(lo, hi):
             half, first = divmod(lo, HALF)
@@ -131,136 +114,147 @@ def tile_list_converter_fault_match_kernel(
             for q in (0, 2, 1, 3):
                 nc.sync.dma_start(wgs_sb[half][32 * q : 32 * (q + 1), :, first : first + hi - lo], src)
 
-        ac_bank = [psum.tile([P, BANK], F32, name=f"ac_bank{i}") for i in range(UNITS)]
-        b_bank = [psum.tile([P, BANK], F32, name=f"b_bank{i}") for i in range(UNITS)]
-        a_sb = [sbuf(f"a_sb{i}", [P, BANK], F32) for i in range(RA)]
-        c_sb = [pair[i // 2][:, (i % 2) * BANK : (i % 2 + 1) * BANK] for i in range(UNITS)]
-        m_sb = [sbuf(f"m_sb{i}", [P, BANK], F32) for i in range(RM)]
-        w_sb = [sbuf(f"w_sb{i}", [P, BANK], F32) for i in range(3)]
-        h_sb = [sbuf(f"h_sb{i}", [P, PACK, HALF], F32) for i in range(2)]
+        def gather_table(dst, window, half):
+            lo, hi = half * HALF, (half + 1) * HALF
+            nc.vector.tensor_copy(dst[:, lo:hi], window.indirect(entries(pick, lo, hi)))
 
+        def weave_weight(i, copy, lo, hi):
+            if i == 0:
+                dst = woven[i][:].rearrange("p (u m e) j -> p m j u e", u=2, e=2)
+                src = raw[i][:].rearrange("p j (m u e) -> p m j u e", u=2, e=2)
+            else:
+                dst = woven[i][:].rearrange("p (t m) j -> p m j t", t=PACK)
+                src = raw[i][:].rearrange("p j (m t) -> p m j t", t=PACK)
+            copy(dst[:, lo:hi], src[:, lo:hi])
 
-        def product(bank, phase, k, codes, plane):
-            half = phase % 2
-            tok = slice(half * HALF + k * P, half * HALF + (k + 1) * P)
-            nc.tensor.matmul_mx(
-                out=bank[:], lhsT=v_w[:, tok].bitcast(FP8X4), lhsT_scale=v_s[:, tok],
-                rhs=codes, rhs_scale=plane, start=True, stop=True,
-            )
+        def quantise(codes, scales, src):
+            nc.vector.quantize_mx(out=codes.bitcast(FP8X4), scales=scales, in_=src.rearrange("p c t -> p (c t)"))
 
-        def float_product(i, phase, k, dst, copy):
-            b = phase // 2
+        def quantise_weight(i, b):
             cols = slice(b * BANK, (b + 1) * BANK)
-            bank = ac_bank[2 * i + k % 2]
-            product(bank, phase, k, w_codes[i][:, cols].bitcast(FP8X4), w_planes[i][:, cols])
-            copy(dst, bank[:])
+            quantise(w_codes[i][:, cols], w_scales[i][:, cols], woven[i][:])
 
-        def packed_product(phase, k):
-            b = phase // 2
-            product(
-                b_bank[k], phase, k,
-                wb_w[:, 2 * b * BANK : 2 * (b + 1) * BANK].bitcast(FP4X4), wb_s[:, b * BANK : (b + 1) * BANK],
+        def product(bank, unit, codes, scales):
+            first = (unit % (2 * UNITS)) * P
+            picked = slice(first, first + P)
+            nc.tensor.matmul_mx(
+                out=bank[:], lhsT=v_w[:, picked].bitcast(FP8X4), lhsT_scale=v_s[:, picked],
+                rhs=codes, rhs_scale=scales, start=True, stop=True,
             )
+
+        def float_product(i, unit, bank, dst, copy):
+            b = unit // (2 * UNITS)
+            cols = slice(b * BANK, (b + 1) * BANK)
+            product(bank, unit, w_codes[i][:, cols].bitcast(FP8X4), w_scales[i][:, cols])
+            copy(dst, bank[:])
 
         def by_pair(buf):
             return buf[:].rearrange("j (u m e) -> j u m e", u=2, e=2)
 
-        def maximum(u):
-            natural = b_bank[u % UNITS][:].rearrange("j (m u e) -> j u m e", u=2, e=2)
-            nc.vector.tensor_tensor(by_pair(m_sb[u % RM]), natural, by_pair(a_sb[u % RA]), ALU.max)
+        def larger(unit):
+            b, k = unit // (2 * UNITS), unit % UNITS
+            words = wb_w[:, 2 * b * BANK : 2 * (b + 1) * BANK].bitcast(FP4X4)
+            product(b_bank[k], unit, words, wb_s[:, b * BANK : (b + 1) * BANK])
+            a = a_sb[unit % A_BUFS]
+            float_product(0, unit, a_bank[unit % 2], a[:], nc.scalar.copy)
+            as_arrived = b_bank[k][:].rearrange("j (m u e) -> j u m e", u=2, e=2)
+            nc.vector.tensor_tensor(by_pair(m_sb[k]), as_arrived, by_pair(a), ALU.max)
 
-        def bend(u):
-            phase, k = divmod(u, UNITS)
-            z = ac_bank[2 + k % 2][:].rearrange("p (t j) -> p t j", t=PACK)
+        def third(unit, copy):
+            float_product(1, unit, c_bank[unit % 2], c_sb[unit % UNITS], copy)
+
+        def bend(unit):
+            half, k = (unit // UNITS) % 2, unit % UNITS
+            z = c_bank[unit % 2][:].rearrange("p (t j) -> p t j", t=PACK)
             for t in range(PACK):
                 nc.tensor.matmul(
-                    z[:, t, :], c_sb[u % UNITS][:, t * P : (t + 1) * P], ident[:],
+                    z[:, t, :], c_sb[k][:, t * P : (t + 1) * P], ident[:],
                     start=(t == 0), stop=False, is_transpose=True,
                 )
             for t in range(PACK):
                 nc.tensor.matmul(
-                    z[:, t, :], by_pair(m_sb[u % RM])[:, t // 2, :, t % 2], ident[:],
+                    z[:, t, :], by_pair(m_sb[k])[:, t // 2, :, t % 2], ident[:],
                     start=False, stop=(t == PACK - 1), is_transpose=True,
                 )
-            nc.scalar.activation(h_sb[phase % 2][:, :, k * P : (k + 1) * P], z, ACT.Tanh)
+            nc.scalar.activation(h_sb[half][:, :, k * P : (k + 1) * P], z, ACT.Tanh)
 
-        def larger(u):
-            packed_product(u // UNITS, u % UNITS)
-            float_product(0, u // UNITS, u % UNITS, a_sb[u % RA][:], nc.scalar.copy)
-            maximum(u)
+        def weigh_on_scalar(b, t, lo, hi, factor):
+            half, first = divmod(lo, HALF)
+            rows = wgs_sb[half][:, t, first : first + hi - lo]
+            nc.scalar.activation(factor, rows, ACT.Copy, scale=gain_sb[:, b, t : t + 1])
 
-        def third(u, copy):
-            float_product(1, u // UNITS, u % UNITS, c_sb[u % UNITS], copy)
+        def weigh_on_vector(b, t, lo, hi, factor):
+            half, first = divmod(lo, HALF)
+            rows = wgs_sb[half][:, t, first : first + hi - lo]
+            nc.vector.tensor_scalar(factor, rows, gain_sb[:, b, t : t + 1], None, ALU.mult)
 
-        def weigh(phase, t, lo, hi, factor):
-            b, half = divmod(phase, 2)
-            rows = wgs_sb[half][:, t, lo:hi]
-            if hi - lo == QUARTER or (phase, t) == (1, 0):
-                nc.vector.tensor_scalar(factor, rows, gain_sb[:, b, t : t + 1], None, ALU.mult)
-            else:
-                nc.scalar.activation(factor, rows, ACT.Copy, scale=gain_sb[:, b, t : t + 1])
-
-        def scatter(phase, t, lo, hi, factor):
-            b, half = divmod(phase, 2)
+        def scatter(b, t, lo, hi, factor):
+            half, first = divmod(lo, HALF)
             nc.vector.tensor_tensor(
-                page[b, t][:].indirect(put[:, (half * HALF + lo) // 16 : (half * HALF + hi) // 16]),
-                h_sb[phase % 2][:, t, lo:hi], factor, ALU.mult,
+                page[b, t][:].indirect(entries(put, lo, hi)),
+                h_sb[half][:, t, first : first + hi - lo], factor, ALU.mult,
             )
 
-        g1 = [sbuf("g1", [P, PACK, NP], F32), raw[0]]
-        g2 = [sbuf(f"g2_{i}", [P, NP], F32) for i in range(PACK)]
-        y2 = [sbuf("y2_0", [P, PACK, NP], BF16, "late"), sbuf("y2_1", [P, PACK, NP], BF16)]
-        x_codes = [[sbuf(f"x_codes0{b}", [P, NP], U32) for b in range(PASSES)]]
-        last_factor = sbuf("last_factor", [P, HALF], F32, "late")
-        x_codes.append([sbuf("x_codes10", [P, NP], U32, "late"), sbuf("x_codes11", [P, NP], U32)])
-        x_planes = [[sbuf(f"x_planes{i}{b}", [P, NP], U8) for b in range(PASSES)] for i in range(2)]
+        def fetch_x2(b, t, lo, hi):
+            nc.vector.tensor_copy(x2_picked[t][:, lo:hi], page[b, t][:].indirect(entries(protos, lo, hi)))
+
+        def fetch_x1(b, t, dst):
+            nc.vector.tensor_copy(dst, page[b, t][:].indirect(beds[:]))
 
         def fetch(b, t):
-            direct = b == PASSES - 1 and t >= 2
-            nc.vector.tensor_copy(g2[t][:], page[b, t][:].indirect(protos[:]))
-            nc.vector.tensor_copy(x_woven[0][:, :, t] if direct else g1[b][:, t, :], page[b, t][:].indirect(beds[:]))
+            fetch_x2(b, t, 0, NP)
+            fetch_x1(b, t, x1_rows[b][:, t, :])
 
-        def centre(b, t):
-            last = b == PASSES - 1 and t == PACK - 1
+        def centre(b, t, lo, hi, dst):
             nc.scalar.activation(
-                x_woven[1][:, :, t] if last else y2[b][:, t, :], g2[t][:], ACT.Identity,
-                bias=shift[:, b, t : t + 1], scale=wr_sb[:, b, t : t + 1],
+                dst, x2_picked[t][:, lo:hi], ACT.Identity, bias=shift[:, b, t : t + 1], scale=wr_sb[:, b, t : t + 1]
             )
 
-        def quantise_x(i, b, src):
-            nc.vector.quantize_mx(
-                out=x_codes[i][b][:].bitcast(FP8X4), scales=x_planes[i][b][:],
-                in_=src.rearrange("p c t -> p (c t)"),
-            )
+        def weave_rows(dst, src):
+            nc.scalar.copy(dst.rearrange("p (c i) t -> p c t i", i=4), src.rearrange("p t (c i) -> p c t i", i=4))
 
         def score(b, c):
             rows = slice(c * P, (c + 1) * P)
             nc.tensor.matmul_mx(
-                out=b_bank[c][:], lhsT=x_codes[0][b][:, rows].bitcast(FP8X4), lhsT_scale=x_planes[0][b][:, rows],
-                rhs=x_codes[1][b][:].bitcast(FP8X4), rhs_scale=x_planes[1][b][:],
+                out=b_bank[c][:], lhsT=x_codes[0][b][:, rows].bitcast(FP8X4), lhsT_scale=x_scales[0][b][:, rows],
+                rhs=x_codes[1][b][:].bitcast(FP8X4), rhs_scale=x_scales[1][b][:],
                 start=(b == 0), stop=(b == PASSES - 1),
             )
 
-        load_plane(wb_s, wb_scales, nc.gpsimd, nc.gpsimd)
+        nc.sync.dma_start(pick[:], offs)
+        make_identity(nc, ident[:])
         load_weight(0, 0)
         load_weight(1, 0)
         nc.sync.dma_start(wb_w[:].bitcast(I32), wb_words[0].bitcast(I32))
         nc.sync.dma_start(put[:], offs2)
-        load_plane(tab_s, tab_scales, nc.vector, nc.sync)
+        load_scales(tab_s, tab_scales, nc.vector)
         nc.sync.dma_start(tab_w[:], tab_words[0].rearrange("p t i -> p (t i)").bitcast(I32))
-        gain_sb = load_rows("gain_sb", gain)
-        QUARTER = HALF // 2
+        load_scales(wb_s, wb_scales, nc.gpsimd)
+        gain_sb = load_by_row("gain_sb", gain)
         load_page(0, 0)
         load_wgs(0, QUARTER)
         load_page(0, 1)
         load_wgs(QUARTER, HALF)
+
+        warm = sbuf("warm", [P, 1], F32)
+        nc.scalar.activation(warm[:], raw[0][:, 0, 0:1], ACT.Tanh)
+
         for i in range(2):
-            weave_weight(i, nc.vector.tensor_copy, 0, BANK // 2)
-            weave_weight(i, nc.scalar.copy, BANK // 2, BANK)
+            weave_weight(i, nc.vector.tensor_copy, 0, P // 2)
+            weave_weight(i, nc.scalar.copy, P // 2, P)
             quantise_weight(i, 0)
-        gather_words(0)
+        gather_table(v_s, tab_s[:], 0)
+        gather_table(v_s, tab_s[:], 1)
+
+        for n in range(WARM_PASSES):
+            nc.tensor.matmul_mx(
+                out=b_bank[3][:], lhsT=w_codes[0][:, 0:P].bitcast(FP8X4), lhsT_scale=v_s[:, HALF : HALF + P],
+                rhs=w_codes[1][:, 0:BANK].bitcast(FP8X4), rhs_scale=w_scales[1][:, 0:BANK], start=True, stop=True,
+            )
+
+        gather_table(v_w, tab_w[:].bitcast(U32), 0)
         larger(0)
-        third(0, nc.scalar.copy)
+        third(0, nc.vector.tensor_copy)
         larger(1)
         nc.sync.dma_start(beds[:], offs3)
         nc.sync.dma_start(protos[:], offs4)
@@ -269,100 +263,112 @@ def tile_list_converter_fault_match_kernel(
         load_wgs(HALF, S)
         load_weight(0, 1)
         load_weight(1, 1)
-        base_sb = load_rows("base_sb", base)
-        wr_sb = load_rows("wr_sb", wr)
-        third(1, nc.vector.tensor_copy)
+        base_sb = load_by_row("base_sb", base)
+        wr_sb = load_by_row("wr_sb", wr)
+        third(1, nc.scalar.copy)
         bend(0)
         bend(1)
-        gather_words(1)
+        gather_table(v_w, tab_w[:].bitcast(U32), 1)
         shift = sbuf("shift", [P, PASSES, PACK], F32)
         nc.vector.scalar_tensor_tensor(shift[:], base_sb[:], -1.0, wr_sb[:], ALU.mult, ALU.mult)
 
-        PLAN = {0: [("l", 2), ("t", 2), ("l", 3), ("b", 2)], 1: [("t", 3), ("b", 3)]}
-        for i in range(2, 6):
-            PLAN[i] = [("l", i + 2), ("t", i + 2), ("b", i + 2)]
-        PLAN[8] = [("l", 8), ("l", 9), ("l", 10), ("l", 11), ("t", 8), ("t", 9)]
-        PLAN[9] = [("b", 8), ("w", 0), ("t", 10), ("b", 9), ("t", 11), ("l", 12)]
-        PLAN[10] = [("b", 10), ("t", 12), ("b", 11), ("w", 0), ("l", 13), ("t", 13), ("b", 12)]
-        for i in range(11, 13):
-            PLAN[i] = [("l", i + 3), ("t", i + 3), ("b", i + 2)]
-        PLAN[13] = [("b", 15)]
-        steps = [(0, t, lo, lo + QUARTER) for lo in (0, QUARTER) for t in range(2)]
-        steps = steps + [(0, t, 0, HALF) for t in range(2, PACK)]
-        steps = steps + [(phase, t, 0, HALF) for phase in range(1, PHASES) for t in range(PACK)]
-        for i, (phase, t, lo, hi) in enumerate(steps):
-            b, half = divmod(phase, 2)
-            if 1 <= i <= 4:
-                factor = m_sb[i - 1][:, 0 : hi - lo]
-            elif i in (7, 8):
-                factor = raw[i - 7][:, 0, :]
-            elif i == 9:
-                factor = c_sb[0]
-            elif 10 <= i <= 14:
-                factor = m_sb[(i + 1) % RM][:]
-            elif i == 17:
-                factor = last_factor[:]
+        first_half = [(t, lo, lo + QUARTER) for lo in (0, QUARTER) for t in range(2)]
+        first_half = first_half + [(t, 0, HALF) for t in range(2, PACK)]
+        holds = [spare[0]] + m_sb + [spare[2]]
+        for n, (t, lo, hi) in enumerate(first_half):
+            factor = holds[n][:, 0 : hi - lo]
+            weigh = weigh_on_vector if hi - lo == QUARTER else weigh_on_scalar
+            weigh(0, t, lo, hi, factor)
+            if n == 0:
+                larger(2)
+                third(2, nc.scalar.copy)
+                larger(3)
+            elif n == 1:
+                third(3, nc.scalar.copy)
             else:
-                factor = w_sb[FREE[i]][:, 0 : hi - lo]
-            early = i in (0, 1, 2, 3, 4, 5, 6, 11, 12, 13, 14)
-            if early:
-                weigh(phase, t, lo, hi, factor)
-            if i in (7, 8):
-                weave_weight(i - 7, nc.scalar.copy, 0, BANK)
-                quantise_weight(i - 7, 1)
-            for kind, u in PLAN.get(i, ()):
-                if kind == "l":
-                    larger(u)
-                elif kind == "t":
-                    third(u, nc.scalar.copy)
-                elif kind == "w":
-                    weigh(phase, t, lo, hi, factor)
-                else:
-                    bend(u)
-            if phase == 1:
-                load_page(1, t)
-            if i == 15:
-                for n, src in enumerate((g1[0], y2[0])):
-                    weave(nc.scalar.copy, woven[n], src[:])
-                quantise_x(0, 0, woven[0])
-                weigh(3, 3, 0, HALF, last_factor[:])
-            if not early and i not in (9, 10, 17):
-                weigh(phase, t, lo, hi, factor)
-            if i in (CS, CS + 1, CS + 2, CS + 3):
-                centre(0, i - CS)
-            if i in (16, 17):
-                centre(1, i - 16)
-            if i == 17:
-                fetch(1, 2)
-                centre(1, 2)
-                nc.scalar.copy(x_woven[0][:, :, 0:2], g1[1][:, 0:2, :].rearrange("p t c -> p c t"))
-                nc.scalar.copy(x_woven[1][:, :, 0:3], y2[1][:, 0:3, :].rearrange("p t c -> p c t"))
-            scatter(phase, t, lo, hi, factor)
-            if i in (7, 8, 9, 10):
-                fetch(0, i - 7)
-            if i in (15, 16):
-                fetch(1, i - 15)
-        for n in range(2):
-            cols = slice(n * QUARTER, (n + 1) * QUARTER)
-            nc.vector.tensor_copy(g2[3][:, cols], page[1, 3][:].indirect(protos[:, 16 * n : 16 * (n + 1)]))
-            nc.scalar.activation(
-                x_woven[1][:, cols, 3], g2[3][:, cols], ACT.Identity, bias=shift[:, 1, 3:4], scale=wr_sb[:, 1, 3:4]
-            )
-        quantise_x(1, 0, woven[1])
+                larger(n + 2)
+                third(n + 2, nc.scalar.copy)
+            bend(n + 2)
+            scatter(0, t, lo, hi, factor)
+
+        weigh_on_vector(0, 0, HALF, S, spare[0][:])
+        load_page(1, 0)
+        scatter(0, 0, HALF, S, spare[0][:])
+        for i in range(2):
+            t = i + 1
+            weave_weight(i, nc.scalar.copy, 0, P)
+            quantise_weight(i, 1)
+            if i == 1:
+                for unit in range(8, 12):
+                    larger(unit)
+                third(8, nc.scalar.copy)
+                third(9, nc.scalar.copy)
+            load_page(1, t)
+            weigh_on_scalar(0, t, HALF, S, raw[i][:, 0, :])
+            scatter(0, t, HALF, S, raw[i][:, 0, :])
+            fetch(0, t - 1)
+        bend(8)
+        weigh_on_scalar(0, 3, HALF, S, c_sb[0])
+        third(10, nc.scalar.copy)
+        bend(9)
+        third(11, nc.scalar.copy)
+        larger(12)
+        load_page(1, 3)
+        scatter(0, 3, HALF, S, c_sb[0])
+        fetch(0, 2)
+
+        bend(10)
+        third(12, nc.scalar.copy)
+        bend(11)
+        for t in range(PACK):
+            factor = m_sb[(11 + t) % UNITS][:]
+            weigh_on_scalar(1, t, 0, HALF, factor)
+            if t < PACK - 1:
+                larger(13 + t)
+                third(13 + t, nc.scalar.copy)
+            bend(12 + t)
+            if t > 0:
+                centre(0, t - 1, 0, NP, x2_rows[0][:, t - 1, :])
+            scatter(1, t, 0, HALF, factor)
+            if t == 0:
+                fetch(0, 3)
+
+        weigh_on_scalar(1, 0, HALF, S, m_sb[3][:])
+        centre(0, 3, 0, NP, x2_rows[0][:, 3, :])
+        scatter(1, 0, HALF, S, m_sb[3][:])
+        first_woven = [buf[:].bitcast(BF16).rearrange("p (c t) -> p c t", t=PACK) for buf in c_pair]
+        weave_rows(first_woven[0], x1_rows[0][:])
+        weave_rows(first_woven[1], x2_rows[0][:])
+        quantise(x_codes[0][0][:], x_scales[0][0][:], first_woven[0])
+        weigh_on_scalar(1, 3, HALF, S, last_factor[:])
+        for t in range(1, 3):
+            weigh_on_scalar(1, t, HALF, S, spare[t][:])
+            if t == 2:
+                centre(1, 0, 0, NP, x2_rows[1][:, 0, :])
+            scatter(1, t, HALF, S, spare[t][:])
+            fetch(1, t - 1)
+        centre(1, 1, 0, NP, x2_rows[1][:, 1, :])
+        fetch_x2(1, 2, 0, NP)
+        fetch_x1(1, 2, woven[0][:, :, 2])
+        centre(1, 2, 0, NP, x2_rows[1][:, 2, :])
+        nc.scalar.copy(woven[0][:, :, 0:2], x1_rows[1][:, 0:2, :].rearrange("p t c -> p c t"))
+        nc.scalar.copy(woven[1][:, :, 0:3], x2_rows[1][:].rearrange("p t c -> p c t"))
+        scatter(1, 3, HALF, S, last_factor[:])
+
+        halves = [(0, NP // 2), (NP // 2, NP)]
+        for lo, hi in halves:
+            fetch_x2(1, 3, lo, hi)
+            centre(1, 3, lo, hi, woven[1][:, lo:hi, 3])
+        quantise(x_codes[1][0][:], x_scales[1][0][:], first_woven[1])
         for c in range(UNITS):
             score(0, c)
-        nc.vector.tensor_copy(x_woven[0][:, :, 3], page[1, 3][:].indirect(beds[:]))
-
+        fetch_x1(1, 3, woven[0][:, :, 3])
         bed_sb = sbuf("bed_sb", [P, UNITS], F32)
         with nc.allow_non_contiguous_dma(reason="one offset for each output row"):
             nc.sync.dma_start(bed_sb[:], bed.rearrange("(c p) -> p c", p=P))
-        quantise_x(1, 1, x_woven[1][:])
-        for n in range(2):
-            cols = slice(n * QUARTER, (n + 1) * QUARTER)
-            nc.vector.quantize_mx(
-                out=x_codes[0][1][:, cols].bitcast(FP8X4), scales=x_planes[0][1][:, cols],
-                in_=x_woven[0][:, cols, :].rearrange("p c t -> p (c t)"),
-            )
+        quantise(x_codes[1][1][:], x_scales[1][1][:], woven[1][:])
+        for lo, hi in halves:
+            quantise(x_codes[0][1][:, lo:hi], x_scales[0][1][:, lo:hi], woven[0][:, lo:hi, :])
         for c in range(UNITS):
             score(1, c)
             res = sbuf(f"res{c}", [P, NP], F32)

from contextlib import ExitStack

import concourse.mybir as mybir
from concourse.masks import make_identity

K, H, T, S, T2, NP = 512, 1024, 4096, 1024, 2048, 512
FLOPS = 2 * (3 * K * H * S + H * NP * NP)

F32 = mybir.dt.float32
BF16 = mybir.dt.bfloat16
I32 = mybir.dt.int32
U32 = mybir.dt.uint32
U16 = mybir.dt.uint16
U8 = mybir.dt.uint8
FP8X4 = mybir.dt.float8_e4m3fn_x4
FP4X4 = mybir.dt.float4_e2m1fn_x4
ALU = mybir.AluOpType
ACT = mybir.ActivationFunctionType

P = 128
PACK = 4
BANK = 512
GROUP = 16
HALF = S // 2
QUARTER = S // 4
PASSES = H // BANK
UNITS = HALF // P
PAGE_BUFS = 6
A_BUFS = 3
WARM_PASSES = 3


def tile_list_converter_fault_match_kernel(
    tc, tab_words, tab_scales, offs, wa, wb_words, wb_scales, wc, gain, page0, wgs,
    offs2, offs3, offs4, base, wr, bed, out,
):
    nc = tc.nc
    with ExitStack() as ctx:
        keep = ctx.enter_context(tc.tile_pool(name="keep", bufs=1))
        pages = ctx.enter_context(tc.tile_pool(name="pages", bufs=PAGE_BUFS))
        psum = ctx.enter_context(tc.psum_pool(name="psum", bufs=1))

        def sbuf(name, shape, dtype, tag=None):
            return keep.tile(shape, dtype, name=name, tag=tag or name, align_bytes=64)

        def entries(offsets, lo, hi):
            return offsets[:, lo // GROUP : hi // GROUP]

        pick = keep.tile([P, S // GROUP], U16, name="pick")
        put = keep.tile([P, S // GROUP], U16, name="put")
        beds = keep.tile([P, NP // GROUP], U16, name="beds")
        protos = keep.tile([P, NP // GROUP], U16, name="protos")

        tab_w = sbuf("tab_w", [P, T], I32)
        tab_s = sbuf("tab_s", [P, T], U8)
        wb_w = sbuf("wb_w", [P, 2 * H], U8)
        wb_s = sbuf("wb_s", [P, H], U8)
        v_w = sbuf("v_w", [P, S], U32)
        v_s = sbuf("v_s", [P, S], U8)
        ident = sbuf("ident", [P, P], F32)

        weights = (wa, wc)
        raw = [sbuf(f"raw{i}", [P, PACK, BANK], F32) for i in range(2)]
        w_codes = [sbuf(f"w_codes{i}", [P, H], U32) for i in range(2)]
        w_scales = [sbuf(f"w_scales{i}", [P, H], U8) for i in range(2)]
        woven = [sbuf(f"woven{i}", [P, BANK, PACK], BF16) for i in range(2)]

        a_bank = [psum.tile([P, BANK], F32, name=f"a_bank{i}") for i in range(2)]
        c_bank = [psum.tile([P, BANK], F32, name=f"c_bank{i}") for i in range(2)]
        b_bank = [psum.tile([P, BANK], F32, name=f"b_bank{i}") for i in range(UNITS)]
        a_sb = [sbuf(f"a_sb{i}", [P, BANK], F32) for i in range(A_BUFS)]
        m_sb = [sbuf(f"m_sb{i}", [P, BANK], F32) for i in range(UNITS)]
        c_pair = [sbuf(f"c_pair{i}", [P, 2 * BANK], F32) for i in range(2)]
        c_sb = [c_pair[k // 2][:, (k % 2) * BANK : (k % 2 + 1) * BANK] for k in range(UNITS)]
        h_sb = [sbuf(f"h_sb{half}", [P, PACK, HALF], F32) for half in range(2)]
        wgs_sb = [sbuf(f"wgs_sb{half}", [P, PACK, HALF], F32) for half in range(2)]
        spare = [sbuf(f"spare{i}", [P, HALF], F32) for i in range(3)]
        page = {}

        x1_rows = [sbuf("x1_rows0", [P, PACK, NP], F32), raw[0]]
        x2_picked = [sbuf(f"x2_picked{t}", [P, NP], F32) for t in range(PACK)]
        x2_rows = [sbuf("x2_rows0", [P, PACK, NP], BF16, "late"), sbuf("x2_rows1", [P, PACK - 1, NP], BF16)]
        last_factor = sbuf("last_factor", [P, HALF], F32, "late")
        x_codes = [
            [sbuf(f"x1_codes{b}", [P, NP], U32) for b in range(PASSES)],
            [sbuf("x2_codes0", [P, NP], U32, "late"), sbuf("x2_codes1", [P, NP], U32)],
        ]
        x_scales = [[sbuf(f"x{i + 1}_scales{b}", [P, NP], U8) for b in range(PASSES)] for i in range(2)]

        def load_scales(plane, src, clearing_engine):
            clearing_engine.memset(plane[:].bitcast(I32), 0)
            for q in range(4):
                nc.sync.dma_start(
                    plane[32 * q : 32 * q + 4, :].bitcast(I32), src[0, 4 * q : 4 * q + 4, :].bitcast(I32)
                )

        def load_weight(i, b):
            rows = weights[i].rearrange("(p t) r -> p t r", t=PACK)
            nc.sync.dma_start(raw[i][:], rows[:, :, b * BANK : (b + 1) * BANK])

        def load_by_row(name, vec):
            buf = sbuf(name, [P, PASSES, PACK], F32)
            nc.sync.dma_start(buf[:], vec.rearrange("(b p t) -> p b t", p=P, t=PACK))
            return buf

        def load_page(b, t):
            buf = pages.tile([P, T2], F32, name="page")
            nc.sync.dma_start(buf[:], page0.rearrange("(b p t) s -> b t p s", p=P, t=PACK)[b, t])
            page[b, t] = buf

        def load_wgs(lo, hi):
            half, first = divmod(lo, HALF)
            src = wgs.rearrange("(m t) j -> m t j", t=PACK)[:, :, lo:hi]
            for q in (0, 2, 1, 3):
                nc.sync.dma_start(wgs_sb[half][32 * q : 32 * (q + 1), :, first : first + hi - lo], src)

        def gather_table(dst, window, half):
            lo, hi = half * HALF, (half + 1) * HALF
            nc.vector.tensor_copy(dst[:, lo:hi], window.indirect(entries(pick, lo, hi)))

        def weave_weight(i, copy, lo, hi):
            if i == 0:
                dst = woven[i][:].rearrange("p (u m e) j -> p m j u e", u=2, e=2)
                src = raw[i][:].rearrange("p j (m u e) -> p m j u e", u=2, e=2)
            else:
                dst = woven[i][:].rearrange("p (t m) j -> p m j t", t=PACK)
                src = raw[i][:].rearrange("p j (m t) -> p m j t", t=PACK)
            copy(dst[:, lo:hi], src[:, lo:hi])

        def quantise(codes, scales, src):
            nc.vector.quantize_mx(out=codes.bitcast(FP8X4), scales=scales, in_=src.rearrange("p c t -> p (c t)"))

        def quantise_weight(i, b):
            cols = slice(b * BANK, (b + 1) * BANK)
            quantise(w_codes[i][:, cols], w_scales[i][:, cols], woven[i][:])

        def product(bank, unit, codes, scales):
            first = (unit % (2 * UNITS)) * P
            picked = slice(first, first + P)
            nc.tensor.matmul_mx(
                out=bank[:], lhsT=v_w[:, picked].bitcast(FP8X4), lhsT_scale=v_s[:, picked],
                rhs=codes, rhs_scale=scales, start=True, stop=True,
            )

        def float_product(i, unit, bank, dst, copy):
            b = unit // (2 * UNITS)
            cols = slice(b * BANK, (b + 1) * BANK)
            product(bank, unit, w_codes[i][:, cols].bitcast(FP8X4), w_scales[i][:, cols])
            copy(dst, bank[:])

        def by_pair(buf):
            return buf[:].rearrange("j (u m e) -> j u m e", u=2, e=2)

        def larger(unit):
            b, k = unit // (2 * UNITS), unit % UNITS
            words = wb_w[:, 2 * b * BANK : 2 * (b + 1) * BANK].bitcast(FP4X4)
            product(b_bank[k], unit, words, wb_s[:, b * BANK : (b + 1) * BANK])
            a = a_sb[unit % A_BUFS]
            float_product(0, unit, a_bank[unit % 2], a[:], nc.scalar.copy)
            as_arrived = b_bank[k][:].rearrange("j (m u e) -> j u m e", u=2, e=2)
            nc.vector.tensor_tensor(by_pair(m_sb[k]), as_arrived, by_pair(a), ALU.max)

        def third(unit, copy):
            float_product(1, unit, c_bank[unit % 2], c_sb[unit % UNITS], copy)

        def bend(unit):
            half, k = (unit // UNITS) % 2, unit % UNITS
            z = c_bank[unit % 2][:].rearrange("p (t j) -> p t j", t=PACK)
            for t in range(PACK):
                nc.tensor.matmul(
                    z[:, t, :], c_sb[k][:, t * P : (t + 1) * P], ident[:],
                    start=(t == 0), stop=False, is_transpose=True,
                )
            for t in range(PACK):
                nc.tensor.matmul(
                    z[:, t, :], by_pair(m_sb[k])[:, t // 2, :, t % 2], ident[:],
                    start=False, stop=(t == PACK - 1), is_transpose=True,
                )
            nc.scalar.activation(h_sb[half][:, :, k * P : (k + 1) * P], z, ACT.Tanh)

        def weigh_on_scalar(b, t, lo, hi, factor):
            half, first = divmod(lo, HALF)
            rows = wgs_sb[half][:, t, first : first + hi - lo]
            nc.scalar.activation(factor, rows, ACT.Copy, scale=gain_sb[:, b, t : t + 1])

        def weigh_on_vector(b, t, lo, hi, factor):
            half, first = divmod(lo, HALF)
            rows = wgs_sb[half][:, t, first : first + hi - lo]
            nc.vector.tensor_scalar(factor, rows, gain_sb[:, b, t : t + 1], None, ALU.mult)

        def scatter(b, t, lo, hi, factor):
            half, first = divmod(lo, HALF)
            nc.vector.tensor_tensor(
                page[b, t][:].indirect(entries(put, lo, hi)),
                h_sb[half][:, t, first : first + hi - lo], factor, ALU.mult,
            )

        def fetch_x2(b, t, lo, hi):
            nc.vector.tensor_copy(x2_picked[t][:, lo:hi], page[b, t][:].indirect(entries(protos, lo, hi)))

        def fetch_x1(b, t, dst):
            nc.vector.tensor_copy(dst, page[b, t][:].indirect(beds[:]))

        def fetch(b, t):
            fetch_x2(b, t, 0, NP)
            fetch_x1(b, t, x1_rows[b][:, t, :])

        def centre(b, t, lo, hi, dst):
            nc.scalar.activation(
                dst, x2_picked[t][:, lo:hi], ACT.Identity, bias=shift[:, b, t : t + 1], scale=wr_sb[:, b, t : t + 1]
            )

        def weave_rows(dst, src):
            nc.scalar.copy(dst.rearrange("p (c i) t -> p c t i", i=4), src.rearrange("p t (c i) -> p c t i", i=4))

        def score(b, c):
            rows = slice(c * P, (c + 1) * P)
            nc.tensor.matmul_mx(
                out=b_bank[c][:], lhsT=x_codes[0][b][:, rows].bitcast(FP8X4), lhsT_scale=x_scales[0][b][:, rows],
                rhs=x_codes[1][b][:].bitcast(FP8X4), rhs_scale=x_scales[1][b][:],
                start=(b == 0), stop=(b == PASSES - 1),
            )

        nc.sync.dma_start(pick[:], offs)
        make_identity(nc, ident[:])
        load_weight(0, 0)
        load_weight(1, 0)
        nc.sync.dma_start(wb_w[:].bitcast(I32), wb_words[0].bitcast(I32))
        nc.sync.dma_start(put[:], offs2)
        load_scales(tab_s, tab_scales, nc.vector)
        nc.sync.dma_start(tab_w[:], tab_words[0].rearrange("p t i -> p (t i)").bitcast(I32))
        load_scales(wb_s, wb_scales, nc.gpsimd)
        gain_sb = load_by_row("gain_sb", gain)
        load_page(0, 0)
        load_wgs(0, QUARTER)
        load_page(0, 1)
        load_wgs(QUARTER, HALF)

        warm = sbuf("warm", [P, 1], F32)
        nc.scalar.activation(warm[:], raw[0][:, 0, 0:1], ACT.Tanh)

        for i in range(2):
            weave_weight(i, nc.vector.tensor_copy, 0, P // 2)
            weave_weight(i, nc.scalar.copy, P // 2, P)
            quantise_weight(i, 0)
        gather_table(v_s, tab_s[:], 0)
        gather_table(v_s, tab_s[:], 1)

        for n in range(WARM_PASSES):
            nc.tensor.matmul_mx(
                out=b_bank[3][:], lhsT=w_codes[0][:, 0:P].bitcast(FP8X4), lhsT_scale=v_s[:, HALF : HALF + P],
                rhs=w_codes[1][:, 0:BANK].bitcast(FP8X4), rhs_scale=w_scales[1][:, 0:BANK], start=True, stop=True,
            )

        gather_table(v_w, tab_w[:].bitcast(U32), 0)
        larger(0)
        third(0, nc.vector.tensor_copy)
        larger(1)
        nc.sync.dma_start(beds[:], offs3)
        nc.sync.dma_start(protos[:], offs4)
        load_page(0, 2)
        load_page(0, 3)
        load_wgs(HALF, S)
        load_weight(0, 1)
        load_weight(1, 1)
        base_sb = load_by_row("base_sb", base)
        wr_sb = load_by_row("wr_sb", wr)
        third(1, nc.scalar.copy)
        bend(0)
        bend(1)
        gather_table(v_w, tab_w[:].bitcast(U32), 1)
        shift = sbuf("shift", [P, PASSES, PACK], F32)
        nc.vector.scalar_tensor_tensor(shift[:], base_sb[:], -1.0, wr_sb[:], ALU.mult, ALU.mult)

        first_half = [(t, lo, lo + QUARTER) for lo in (0, QUARTER) for t in range(2)]
        first_half = first_half + [(t, 0, HALF) for t in range(2, PACK)]
        holds = [spare[0]] + m_sb + [spare[2]]
        for n, (t, lo, hi) in enumerate(first_half):
            factor = holds[n][:, 0 : hi - lo]
            weigh = weigh_on_vector if hi - lo == QUARTER else weigh_on_scalar
            weigh(0, t, lo, hi, factor)
            if n == 0:
                larger(2)
                third(2, nc.scalar.copy)
                larger(3)
            elif n == 1:
                third(3, nc.scalar.copy)
            else:
                larger(n + 2)
                third(n + 2, nc.scalar.copy)
            bend(n + 2)
            scatter(0, t, lo, hi, factor)

        weigh_on_vector(0, 0, HALF, S, spare[0][:])
        load_page(1, 0)
        scatter(0, 0, HALF, S, spare[0][:])
        for i in range(2):
            t = i + 1
            weave_weight(i, nc.scalar.copy, 0, P)
            quantise_weight(i, 1)
            if i == 1:
                for unit in range(8, 12):
                    larger(unit)
                third(8, nc.scalar.copy)
                third(9, nc.scalar.copy)
            load_page(1, t)
            weigh_on_scalar(0, t, HALF, S, raw[i][:, 0, :])
            scatter(0, t, HALF, S, raw[i][:, 0, :])
            fetch(0, t - 1)
        bend(8)
        weigh_on_scalar(0, 3, HALF, S, c_sb[0])
        third(10, nc.scalar.copy)
        bend(9)
        third(11, nc.scalar.copy)
        larger(12)
        load_page(1, 3)
        scatter(0, 3, HALF, S, c_sb[0])
        fetch(0, 2)

        bend(10)
        third(12, nc.scalar.copy)
        bend(11)
        for t in range(PACK):
            factor = m_sb[(11 + t) % UNITS][:]
            weigh_on_scalar(1, t, 0, HALF, factor)
            if t < PACK - 1:
                larger(13 + t)
                third(13 + t, nc.scalar.copy)
            bend(12 + t)
            if t > 0:
                centre(0, t - 1, 0, NP, x2_rows[0][:, t - 1, :])
            scatter(1, t, 0, HALF, factor)
            if t == 0:
                fetch(0, 3)

        weigh_on_scalar(1, 0, HALF, S, m_sb[3][:])
        centre(0, 3, 0, NP, x2_rows[0][:, 3, :])
        scatter(1, 0, HALF, S, m_sb[3][:])
        first_woven = [buf[:].bitcast(BF16).rearrange("p (c t) -> p c t", t=PACK) for buf in c_pair]
        weave_rows(first_woven[0], x1_rows[0][:])
        weave_rows(first_woven[1], x2_rows[0][:])
        quantise(x_codes[0][0][:], x_scales[0][0][:], first_woven[0])
        weigh_on_scalar(1, 3, HALF, S, last_factor[:])
        for t in range(1, 3):
            weigh_on_scalar(1, t, HALF, S, spare[t][:])
            if t == 2:
                centre(1, 0, 0, NP, x2_rows[1][:, 0, :])
            scatter(1, t, HALF, S, spare[t][:])
            fetch(1, t - 1)
        centre(1, 1, 0, NP, x2_rows[1][:, 1, :])
        fetch_x2(1, 2, 0, NP)
        fetch_x1(1, 2, woven[0][:, :, 2])
        centre(1, 2, 0, NP, x2_rows[1][:, 2, :])
        nc.scalar.copy(woven[0][:, :, 0:2], x1_rows[1][:, 0:2, :].rearrange("p t c -> p c t"))
        nc.scalar.copy(woven[1][:, :, 0:3], x2_rows[1][:].rearrange("p t c -> p c t"))
        scatter(1, 3, HALF, S, last_factor[:])

        halves = [(0, NP // 2), (NP // 2, NP)]
        for lo, hi in halves:
            fetch_x2(1, 3, lo, hi)
            centre(1, 3, lo, hi, woven[1][:, lo:hi, 3])
        quantise(x_codes[1][0][:], x_scales[1][0][:], first_woven[1])
        for c in range(UNITS):
            score(0, c)
        fetch_x1(1, 3, woven[0][:, :, 3])
        bed_sb = sbuf("bed_sb", [P, UNITS], F32)
        with nc.allow_non_contiguous_dma(reason="one offset for each output row"):
            nc.sync.dma_start(bed_sb[:], bed.rearrange("(c p) -> p c", p=P))
        quantise(x_codes[1][1][:], x_scales[1][1][:], woven[1][:])
        for lo, hi in halves:
            quantise(x_codes[0][1][:, lo:hi], x_scales[0][1][:, lo:hi], woven[0][:, lo:hi, :])
        for c in range(UNITS):
            score(1, c)
            res = sbuf(f"res{c}", [P, NP], F32)
            if c % 2 == 0:
                nc.scalar.activation(res[:], b_bank[c][:], ACT.Identity, bias=bed_sb[:, c : c + 1])
            else:
                nc.vector.tensor_scalar(res[:], b_bank[c][:], bed_sb[:, c : c + 1], None, ALU.add)
            nc.sync.dma_start(out[c * P : (c + 1) * P, :], res[:])
